import numpy as np
import ml_dtypes


def mxq(x, axis, fmt="e4m3"):
    dtype, down = {"e4m3": (ml_dtypes.float8_e4m3fn, 7), "e5m2": (ml_dtypes.float8_e5m2, 14)}[fmt]
    v = np.moveaxis(np.asarray(x, np.float32).astype(ml_dtypes.bfloat16).astype(np.float64), axis, -1)
    blocks = v.reshape(v.shape[:-1] + (-1, 32))
    amax = np.abs(blocks).max(-1, keepdims=True)
    byte = np.maximum(np.where(amax > 0, np.frexp(amax)[1] - 1 + 127, 0) - down, 1)
    scale = np.exp2(byte - 127.0)
    codes = (blocks / scale).astype(np.float32).astype(dtype).astype(np.float64)
    return np.moveaxis((codes * scale).reshape(v.shape), -1, axis)


WIDE = False


def mx_kscale(k):
    if not WIDE:
        return np.ones(k)
    levels = np.array([10, -10, 5, -5, 0])
    if k % 512:
        return np.exp2(np.random.permutation(np.resize(levels, k // 32))).repeat(32)
    a = np.empty((k // 512, 16))
    for p in range(k // 512):
        a[p, :8] = np.random.permutation(np.resize(levels, 8))
        for g in range(8):
            far = levels[np.abs(levels - a[p, g]) >= 10]
            a[p, g + 8] = far[np.random.randint(len(far))]
    return np.exp2(a.ravel()).repeat(32)


def f64(x):
    return np.asarray(x).astype(np.float64)


def striped(idx):
    return np.tile(idx.reshape(-1, 16).T, (8, 1)).astype(np.uint16)


def unstriped(offs):
    return offs[:16].T.reshape(-1).astype(np.int64)


def pack_weight(w):
    k, n = w.shape
    w = f64(np.asarray(w, np.float32).astype(ml_dtypes.bfloat16)).reshape(k // 32, 32, n)
    amax = np.abs(w).max(1)
    byte = np.clip(np.where(amax > 0, np.frexp(amax)[1] - 1 + 127 - 7, 1), 1, 254)
    scaled = (w * np.exp2(127.0 - byte)[:, None, :]).reshape(k, n).astype(np.float32)
    words = np.ascontiguousarray(scaled.reshape(k // 512, 128, 4, n).transpose(0, 1, 3, 2)).astype(ml_dtypes.float8_e4m3fn).view(np.uint8)
    return words, np.ascontiguousarray(byte.astype(np.uint8).reshape(k // 512, 16, n))


def unpack_weight(words, scales):
    g, p, n, _ = words.shape
    vals = np.ascontiguousarray(words).view(ml_dtypes.float8_e4m3fn).astype(np.float64) * np.repeat(np.exp2(scales.astype(np.float64) - 127.0), 8, axis=1)[..., None]
    return vals.transpose(0, 1, 3, 2).reshape(g * 512, n)


K, T, S, V, D, G = 512, 2048, 512, 512, 4, 128
P = 2 ** 7


def setup_inputs():
    n = np.random.standard_normal
    s = mx_kscale(K)[:, None]
    packed_xT = pack_weight(n((K, T)) * s)
    return {
        "x_words": packed_xT[0],
        "x_scales": packed_xT[1],
        "hT": (n((K, V)) / np.sqrt(K) / s).astype(np.float32),
        "wgt": (np.tile(np.random.uniform(0.2, 1.5, T), (P, 1))).astype(np.float32),
        "isd0": (np.tile(np.random.uniform(0.1, 0.4, G), (P, 1))).astype(np.float32),
        "isd1": (np.tile(np.random.uniform(0.1, 0.4, G), (P, 1))).astype(np.float32),
        "isd2": (np.tile(np.random.uniform(0.1, 0.4, G), (P, 1))).astype(np.float32),
        "offs": striped(np.random.permutation(T)[:S]),
    }


def reference(x_words, x_scales, hT, wgt, isd0, isd1, isd2, offs):
    hTq = mxq(f64(hT), 0, "e4m3")
    xq = unpack_weight(x_words, x_scales)[:, unstriped(offs)]
    y = (hTq.T @ xq) * (f64(wgt)[:1][:, unstriped(offs)])
    y2 = (y) ** 2
    skat = y2.reshape(len(y2), -1, D).sum(axis=2)
    bur = (y.reshape(len(y), -1, D).sum(axis=2)) ** 2
    z0 = (0.9 * skat + 0.1 * bur - 4.0) * f64(isd0)[:1]
    z1 = (0.5 * skat + 0.5 * bur - 4.0) * f64(isd1)[:1]
    z2 = (0.1 * skat + 0.9 * bur - 4.0) * f64(isd2)[:1]
    return np.log((np.exp(z0) + np.exp(z1) + np.exp(z2)) / 3)

@@ -1,0 +1,238 @@
+import math
+from contextlib import ExitStack
+
+import concourse.mybir as mybir
+from concourse.masks import make_identity
+
+K, T, S, V, D, G = 512, 2048, 512, 512, 4, 128
+P = 128
+PACK = 4
+HALVES = 2
+H = V // HALVES
+
+FLOPS = 2 * K * V * S
+BYTES = K * T + 16 * T + 4 * K * V + 4 * T + 3 * 4 * G + 2 * P * (S // 16) + 4 * V * G
+
+F32 = mybir.dt.float32
+BF16 = mybir.dt.bfloat16
+I32 = mybir.dt.int32
+U32 = mybir.dt.uint32
+U16 = mybir.dt.uint16
+U8 = mybir.dt.uint8
+FP8X4 = mybir.dt.float8_e4m3fn_x4
+ALU = mybir.AluOpType
+ACT = mybir.ActivationFunctionType
+
+
+def tile_picked_yskat_lse_p_kernel(
+    tc, x_words, x_scales, hT, wgt, isd0, isd1, isd2, offs, out
+):
+    nc = tc.nc
+    with ExitStack() as ctx:
+        keep = ctx.enter_context(tc.tile_pool(name="keep", bufs=1))
+        psum = ctx.enter_context(tc.psum_pool(name="psum", bufs=1))
+
+        def sb(name, shape, dtype=F32):
+            return keep.tile(shape, dtype, name=name, align_bytes=64)
+
+        def bank(name, number, shape):
+            return psum.tile(shape, F32, name=name, tag="bank%d" % number)
+
+        halves = range(HALVES)
+
+        offsets = keep.tile([P, S // 16], U16, name="offsets")
+        nc.sync.dma_start(offsets[:], offs)
+
+        scale_table = sb("scale_table", [P, T], U8)
+        nc.vector.memset(scale_table[:].bitcast(I32), 0)
+        for q in range(4):
+            nc.scalar.dma_start(
+                scale_table[32 * q : 32 * q + 4, :].bitcast(I32), x_scales[0, 4 * q : 4 * q + 4, :].bitcast(I32)
+            )
+        weight_table = sb("weight_table", [P, T])
+        nc.vector.memset(weight_table[:], 0.0)
+        nc.scalar.dma_start(weight_table[0:1, :], wgt[0:1, :])
+
+        h_rows = hT.rearrange("(p j) t -> p j t", j=PACK)
+        h_raw = []
+        for h in halves:
+            raw = sb("h_raw%d" % h, [P, PACK, H])
+            nc.sync.dma_start(raw[:], h_rows[:, :, h * H : (h + 1) * H])
+            h_raw.append(raw)
+        word_table = sb("word_table", [P, T], U32)
+        nc.sync.dma_start(word_table[:].bitcast(I32), x_words[0].rearrange("p n t -> p (n t)").bitcast(I32))
+
+        isd = []
+        with nc.allow_non_contiguous_dma(reason="one value a partition"):
+            for i, src in enumerate((isd0, isd1, isd2)):
+                col = sb("isd%d" % i, [P, 1])
+                nc.gpsimd.dma_start(col[:], src[0:1, :].rearrange("o g -> g o"))
+                isd.append(col)
+        ident = sb("ident", [P, P])
+        make_identity(nc, ident[:])
+
+        picked_scales = sb("picked_scales", [P, S], U8)
+        nc.vector.tensor_copy(picked_scales[:], scale_table[:].indirect(offsets[:]))
+        x_scale = sb("x_scale", [P, S], U8)
+        nc.vector.tensor_copy(
+            x_scale[:].rearrange("p (d g) -> p d g", d=D), picked_scales[:].rearrange("p (g d) -> p d g", d=D)
+        )
+        picked_weights = sb("picked_weights", [P, S])
+        nc.vector.tensor_copy(picked_weights[:], weight_table[:].indirect(offsets[:]))
+
+        h_code, h_scale = [], []
+        for h in halves:
+            grouped = sb("h_grouped%d" % h, [P, H, PACK], BF16)
+            nc.scalar.activation(
+                grouped[:].rearrange("p (c i) j -> p c j i", i=4),
+                h_raw[h][:].rearrange("p j (c i) -> p c j i", i=4),
+                ACT.Copy,
+            )
+            code = sb("h_code%d" % h, [P, H], U32)
+            scale = sb("h_scale%d" % h, [P, H], U8)
+            nc.vector.quantize_mx(code[:].bitcast(FP8X4), scale[:], grouped[:].rearrange("p c j -> p (c j)"))
+            h_code.append(code)
+            h_scale.append(scale)
+
+        turned = bank("weights_turned", 7, [P, D, P])
+        for d in range(D):
+            nc.tensor.transpose(turned[:, d, :], picked_weights[:, d:S:D], ident[:])
+        w = sb("w", [P, D])
+        nc.scalar.copy(w[:], turned[:, :, 0])
+
+        def mix(name, terms, constant=0.0):
+            acc = None
+            for n, (factor, col) in enumerate(terms):
+                nxt = sb("%s_%d" % (name, n), [P, 1])
+                if acc is None:
+                    nc.scalar.activation(nxt[:], col[:], ACT.Copy, scale=factor, bias=constant)
+                else:
+                    nc.scalar.activation(nxt[:], col[:], ACT.Identity, scale=factor, bias=acc[:])
+                acc = nxt
+            return acc
+
+        i0, i1, i2 = isd
+        f_skat = mix("f_skat", [(0.9, i0), (-0.1, i2)])
+        f_bur = mix("f_bur", [(0.1, i0), (-0.9, i2)])
+        f_const = mix("f_const", [(-4.0, i0), (4.0, i2)])
+        g_skat = mix("g_skat", [(0.45, i0), (0.05, i2), (-0.5, i1)])
+        g_bur = mix("g_bur", [(0.05, i0), (0.45, i2), (-0.5, i1)])
+        g_const = mix("g_const", [(-4.0, g_skat), (-4.0, g_bur)])
+        z1_factor = mix("z1_factor", [(0.5, i1)])
+        z1_const = mix("z1_const", [(-4.0, i1)], -math.log(3.0))
+
+        x_code = sb("x_code", [P, S], U32)
+        nc.vector.tensor_copy(x_code[:].rearrange("p (d g) -> p g d", d=D), word_table[:].indirect(offsets[:]))
+
+        def wide(name):
+            return [sb("%s%d" % (name, h), [P, H]) for h in halves]
+
+        total = None
+        square = []
+        for d in range(D):
+            running = wide("sum%d_" % d)
+            sq = wide("square%d_" % d)
+            cols = slice(d * G, (d + 1) * G)
+            for h in halves:
+                prod = bank("prod%d%d" % (d, h), HALVES * d + h, [P, H])
+                nc.tensor.matmul_mx(
+                    prod[:],
+                    lhsT=x_code[:, cols].bitcast(FP8X4),
+                    lhsT_scale=x_scale[:, cols],
+                    rhs=h_code[h][:].bitcast(FP8X4),
+                    rhs_scale=h_scale[h][:],
+                    start=True,
+                    stop=True,
+                )
+                if total is None:
+                    nc.vector.tensor_scalar(running[h][:], prod[:], w[:, d : d + 1], None, ALU.mult)
+                else:
+                    nc.vector.scalar_tensor_tensor(
+                        running[h][:], prod[:], w[:, d : d + 1], total[h][:], ALU.mult, ALU.add
+                    )
+                nc.scalar.activation(sq[h][:], prod[:], ACT.Square, scale=w[:, d : d + 1])
+            total = running
+            square.append(sq)
+
+        lo_pair, hi_pair, skat, bur = wide("lo_pair"), wide("hi_pair"), wide("skat"), wide("bur")
+        f_part, g_part, f, g = wide("f_part"), wide("g_part"), wide("f"), wide("g")
+        gap, hi, hi_abs, low_arg = wide("gap"), wide("hi"), wide("hi_abs"), wide("low_arg")
+        e_near, e_low = wide("e_near"), wide("e_low")
+
+        def pair_lo(h):
+            nc.vector.tensor_tensor(lo_pair[h][:], square[0][h][:], square[1][h][:], ALU.add)
+
+        def pair_hi(h):
+            nc.vector.tensor_tensor(hi_pair[h][:], square[2][h][:], square[3][h][:], ALU.add)
+
+        def make_skat(h):
+            nc.vector.tensor_tensor(skat[h][:], lo_pair[h][:], hi_pair[h][:], ALU.add)
+
+        def make_bur(h):
+            nc.scalar.activation(bur[h][:], total[h][:], ACT.Square)
+            nc.scalar.activation(f_part[h][:], bur[h][:], ACT.Identity, scale=f_bur[:], bias=f_const[:])
+            nc.scalar.activation(g_part[h][:], bur[h][:], ACT.Identity, scale=g_bur[:], bias=g_const[:])
+
+        def make_f(h):
+            nc.vector.scalar_tensor_tensor(f[h][:], skat[h][:], f_skat[:], f_part[h][:], ALU.mult, ALU.add)
+            nc.scalar.activation(gap[h][:], f[h][:], ACT.Abs)
+
+        def make_g(h):
+            nc.vector.scalar_tensor_tensor(g[h][:], skat[h][:], g_skat[:], g_part[h][:], ALU.mult, ALU.add)
+
+        def make_hi(h):
+            nc.vector.scalar_tensor_tensor(hi[h][:], gap[h][:], 0.5, g[h][:], ALU.mult, ALU.add)
+            nc.scalar.activation(hi_abs[h][:], hi[h][:], ACT.Abs)
+            nc.scalar.activation(e_near[h][:], hi_abs[h][:], ACT.Exp, scale=-1.0)
+
+        def make_low(h):
+            nc.vector.scalar_tensor_tensor(low_arg[h][:], hi[h][:], 0.0, gap[h][:], ALU.min, ALU.subtract)
+            nc.scalar.activation(e_low[h][:], low_arg[h][:], ACT.Exp)
+
+        pair_lo(0)
+        pair_hi(0)
+        make_bur(0)
+        pair_lo(1)
+        make_skat(0)
+        make_bur(1)
+        pair_hi(1)
+        make_f(0)
+        make_skat(1)
+        make_g(0)
+        make_f(1)
+        make_hi(0)
+        make_g(1)
+        make_low(0)
+        make_hi(1)
+        make_low(1)
+
+        blocks = range(H // P)
+        rest = []
+        for h in halves:
+            acc = bank("rest%d" % h, h, [P, H // P, G])
+            for b in blocks:
+                cols = slice(b * P, (b + 1) * P)
+                nc.tensor.matmul(acc[:, b, :], e_near[h][:, cols], ident[:], start=True, stop=False, is_transpose=True)
+                nc.tensor.matmul(acc[:, b, :], e_low[h][:, cols], ident[:], start=False, stop=True, is_transpose=True)
+            rest.append(acc)
+
+        both, z1, top = wide("both"), wide("z1"), wide("top")
+        for h in halves:
+            nc.vector.tensor_tensor(both[h][:], skat[h][:], bur[h][:], ALU.add)
+        for h in halves:
+            nc.vector.tensor_scalar(z1[h][:], both[h][:], z1_factor[:], z1_const[:], ALU.mult, ALU.add)
+        top_turned = []
+        for h in halves:
+            nc.vector.scalar_tensor_tensor(top[h][:], hi[h][:], 0.0, z1[h][:], ALU.max, ALU.add)
+            acc = bank("top_turned%d" % h, HALVES + h, [P, H // P, G])
+            for b in blocks:
+                nc.tensor.transpose(acc[:, b, :], top[h][:, b * P : (b + 1) * P], ident[:])
+            top_turned.append(acc)
+
+        out_rows = out.rearrange("(h b p) g -> h p b g", h=HALVES, p=P)
+        for h in halves:
+            logs = sb("logs%d" % h, [P, H // P, G])
+            nc.scalar.activation(logs[:], rest[h][:], ACT.Ln, bias=1.0)
+            result = sb("result%d" % h, [P, H // P, G])
+            nc.vector.tensor_tensor(result[:], top_turned[h][:], logs[:], ALU.add)
+            nc.sync.dma_start(out_rows[h], result[:])

@@ -2,7 +2,6 @@ import math
 from contextlib import ExitStack
 
 import concourse.mybir as mybir
-from concourse.masks import make_identity
 
 K, T, S, V, D, G = 512, 2048, 512, 512, 4, 128
 P = 128
@@ -43,33 +42,39 @@ def tile_picked_yskat_lse_p_kernel(
         offsets = keep.tile([P, S // 16], U16, name="offsets")
         nc.sync.dma_start(offsets[:], offs)
 
+        h_rows = hT.rearrange("(p j) t -> p j t", j=PACK)
+        h_raw0 = keep.tile([P, PACK, H], F32, name="h_raw0", tag="h_raw0", align_bytes=64)
+        nc.sync.dma_start(h_raw0[:], h_rows[:, :, 0:H])
+
         scale_table = sb("scale_table", [P, T], U8)
-        nc.vector.memset(scale_table[:].bitcast(I32), 0)
+        nc.gpsimd.memset(scale_table[:].bitcast(I32), 0)
         for q in range(4):
-            nc.scalar.dma_start(
+            nc.sync.dma_start(
                 scale_table[32 * q : 32 * q + 4, :].bitcast(I32), x_scales[0, 4 * q : 4 * q + 4, :].bitcast(I32)
             )
+
+        zero = keep.tile([P, 1], F32, name="zero", tag="word_table", align_bytes=64)
+        nc.vector.memset(zero[:], 0.0)
         weight_table = sb("weight_table", [P, T])
-        nc.vector.memset(weight_table[:], 0.0)
-        nc.scalar.dma_start(weight_table[0:1, :], wgt[0:1, :])
-
-        h_rows = hT.rearrange("(p j) t -> p j t", j=PACK)
-        h_raw = []
-        for h in halves:
-            raw = sb("h_raw%d" % h, [P, PACK, H])
-            nc.sync.dma_start(raw[:], h_rows[:, :, h * H : (h + 1) * H])
-            h_raw.append(raw)
-        word_table = sb("word_table", [P, T], U32)
-        nc.sync.dma_start(word_table[:].bitcast(I32), x_words[0].rearrange("p n t -> p (n t)").bitcast(I32))
-
-        isd = []
-        with nc.allow_non_contiguous_dma(reason="one value a partition"):
-            for i, src in enumerate((isd0, isd1, isd2)):
-                col = sb("isd%d" % i, [P, 1])
-                nc.gpsimd.dma_start(col[:], src[0:1, :].rearrange("o g -> g o"))
-                isd.append(col)
+        nc.vector.tensor_copy(weight_table[:], zero[:].to_broadcast([P, T]))
+        blank = keep.tile([P, P], F32, name="blank", tag="h_raw1", align_bytes=64)
+        nc.vector.tensor_copy(blank[:], zero[:].to_broadcast([P, P]))
         ident = sb("ident", [P, P])
-        make_identity(nc, ident[:])
+        nc.gpsimd.affine_select(
+            out=ident[:],
+            in_=blank[:],
+            compare_op=ALU.not_equal,
+            fill=1.0,
+            base=0,
+            pattern=[[-1, P]],
+            channel_multiplier=1,
+        )
+        nc.sync.dma_start(weight_table[0:1, :], wgt[0:1, :])
+        word_table = keep.tile([P, T], U32, name="word_table", tag="word_table", align_bytes=64)
+        nc.sync.dma_start(word_table[:].bitcast(I32), x_words[0].rearrange("p n t -> p (n t)").bitcast(I32))
+        h_raw1 = keep.tile([P, PACK, H], F32, name="h_raw1", tag="h_raw1", align_bytes=64)
+        nc.sync.dma_start(h_raw1[:], h_rows[:, :, H:V])
+        h_raw = [h_raw0, h_raw1]
 
         picked_scales = sb("picked_scales", [P, S], U8)
         nc.vector.tensor_copy(picked_scales[:], scale_table[:].indirect(offsets[:]))
@@ -81,7 +86,8 @@ def tile_picked_yskat_lse_p_kernel(
         nc.vector.tensor_copy(picked_weights[:], weight_table[:].indirect(offsets[:]))
 
         h_code, h_scale = [], []
-        for h in halves:
+
+        def quantise(h):
             grouped = sb("h_grouped%d" % h, [P, H, PACK], BF16)
             nc.scalar.activation(
                 grouped[:].rearrange("p (c i) j -> p c j i", i=4),
@@ -94,35 +100,55 @@ def tile_picked_yskat_lse_p_kernel(
             h_code.append(code)
             h_scale.append(scale)
 
+        quantise(0)
+
+        isd_all = keep.tile([P, 3, 8], F32, name="isd_all", tag="h_raw0", align_bytes=64)
+        isd = []
+        with nc.allow_non_contiguous_dma(reason="one value a partition"):
+            for i, src in enumerate((isd0, isd1, isd2)):
+                nc.scalar.dma_start(isd_all[:, i, 0:1], src[0:1, :].rearrange("o g -> g o"))
+                isd.append(isd_all[:, i, 0:1])
+
         turned = bank("weights_turned", 7, [P, D, P])
         for d in range(D):
             nc.tensor.transpose(turned[:, d, :], picked_weights[:, d:S:D], ident[:])
-        w = sb("w", [P, D])
-        nc.scalar.copy(w[:], turned[:, :, 0])
-
-        def mix(name, terms, constant=0.0):
-            acc = None
-            for n, (factor, col) in enumerate(terms):
-                nxt = sb("%s_%d" % (name, n), [P, 1])
-                if acc is None:
-                    nc.scalar.activation(nxt[:], col[:], ACT.Copy, scale=factor, bias=constant)
-                else:
-                    nc.scalar.activation(nxt[:], col[:], ACT.Identity, scale=factor, bias=acc[:])
-                acc = nxt
-            return acc
 
         i0, i1, i2 = isd
-        f_skat = mix("f_skat", [(0.9, i0), (-0.1, i2)])
-        f_bur = mix("f_bur", [(0.1, i0), (-0.9, i2)])
-        f_const = mix("f_const", [(-4.0, i0), (4.0, i2)])
-        g_skat = mix("g_skat", [(0.45, i0), (0.05, i2), (-0.5, i1)])
-        g_bur = mix("g_bur", [(0.05, i0), (0.45, i2), (-0.5, i1)])
-        g_const = mix("g_const", [(-4.0, g_skat), (-4.0, g_bur)])
-        z1_factor = mix("z1_factor", [(0.5, i1)])
-        z1_const = mix("z1_const", [(-4.0, i1)], -math.log(3.0))
+        recipes = [
+            ("f_skat", 0.0, [(0.9, i0), (-0.1, i2)]),
+            ("f_bur", 0.0, [(0.1, i0), (-0.9, i2)]),
+            ("f_const", 0.0, [(-4.0, i0), (4.0, i2)]),
+            ("g_skat", 0.0, [(0.45, i0), (0.05, i2), (-0.5, i1)]),
+            ("g_bur", 0.0, [(0.05, i0), (0.45, i2), (-0.5, i1)]),
+            ("g_const", 0.0, [(-2.0, i0), (-2.0, i2), (4.0, i1)]),
+            ("z1_factor", 0.0, [(0.5, i1)]),
+            ("z1_const", -math.log(3.0), [(-4.0, i1)]),
+        ]
+        coef = {}
+        for group in (recipes[0:3], recipes[3:6], recipes[6:8]):
+            for n in range(len(group[0][2])):
+                for name, constant, terms in group:
+                    factor, col = terms[n]
+                    nxt = sb("%s_%d" % (name, n), [P, 1])
+                    so_far = constant if n == 0 else coef[name][:]
+                    nc.gpsimd.tensor_scalar(nxt[:], col, factor, so_far, ALU.mult, ALU.add)
+                    coef[name] = nxt
+        f_skat, f_bur, f_const = coef["f_skat"], coef["f_bur"], coef["f_const"]
+        g_skat, g_bur, g_const = coef["g_skat"], coef["g_bur"], coef["g_const"]
+        z1_factor, z1_const = coef["z1_factor"], coef["z1_const"]
 
         x_code = sb("x_code", [P, S], U32)
-        nc.vector.tensor_copy(x_code[:].rearrange("p (d g) -> p g d", d=D), word_table[:].indirect(offsets[:]))
+        picked_words = sb("picked_words", [P, S], U32)
+        nc.vector.tensor_copy(picked_words[:], word_table[:].indirect(offsets[:]))
+        for pair in range(2):
+            nc.vector.tensor_copy(
+                x_code[:].bitcast(I32).rearrange("p (d g) -> p d g", d=D)[:, 2 * pair : 2 * pair + 2, :],
+                picked_words[:].bitcast(I32).rearrange("p (g d) -> p d g", d=D)[:, 2 * pair : 2 * pair + 2, :],
+            )
+
+        quantise(1)
+        w = keep.tile([P, D], F32, name="w", tag="h_raw1", align_bytes=64)
+        nc.scalar.copy(w[:], turned[:, :, 0])
 
         def wide(name):
             return [sb("%s%d" % (name, h), [P, H]) for h in halves]
@@ -130,7 +156,8 @@ def tile_picked_yskat_lse_p_kernel(
         total = None
         square = []
         for d in range(D):
-            running = wide("sum%d_" % d)
+            total_all = sb("sum%d" % d, [P, V])
+            running = [total_all[:, h * H : (h + 1) * H] for h in halves]
             sq = wide("square%d_" % d)
             cols = slice(d * G, (d + 1) * G)
             for h in halves:
@@ -145,80 +172,60 @@ def tile_picked_yskat_lse_p_kernel(
                     stop=True,
                 )
                 if total is None:
-                    nc.vector.tensor_scalar(running[h][:], prod[:], w[:, d : d + 1], None, ALU.mult)
+                    nc.vector.tensor_scalar(running[h], prod[:], w[:, d : d + 1], None, ALU.mult)
                 else:
                     nc.vector.scalar_tensor_tensor(
-                        running[h][:], prod[:], w[:, d : d + 1], total[h][:], ALU.mult, ALU.add
+                        running[h], prod[:], w[:, d : d + 1], total[h], ALU.mult, ALU.add
                     )
                 nc.scalar.activation(sq[h][:], prod[:], ACT.Square, scale=w[:, d : d + 1])
+            before_last = total
             total = running
             square.append(sq)
 
-        lo_pair, hi_pair, skat, bur = wide("lo_pair"), wide("hi_pair"), wide("skat"), wide("bur")
-        f_part, g_part, f, g = wide("f_part"), wide("g_part"), wide("f"), wide("g")
-        gap, hi, hi_abs, low_arg = wide("gap"), wide("hi"), wide("hi_abs"), wide("low_arg")
-        e_near, e_low = wide("e_near"), wide("e_low")
+        def step(name, emit):
+            tiles = wide(name)
+            for h in halves:
+                emit(tiles[h][:], h)
+            return tiles
 
-        def pair_lo(h):
-            nc.vector.tensor_tensor(lo_pair[h][:], square[0][h][:], square[1][h][:], ALU.add)
+        def add(dst, a, b):
+            nc.vector.tensor_tensor(dst, a, b, ALU.add)
 
-        def pair_hi(h):
-            nc.vector.tensor_tensor(hi_pair[h][:], square[2][h][:], square[3][h][:], ALU.add)
+        def fused(dst, a, scalar, b, op0, op1):
+            nc.vector.scalar_tensor_tensor(dst, a, scalar, b, op0, op1)
 
-        def make_skat(h):
-            nc.vector.tensor_tensor(skat[h][:], lo_pair[h][:], hi_pair[h][:], ALU.add)
-
-        def make_bur(h):
-            nc.scalar.activation(bur[h][:], total[h][:], ACT.Square)
-            nc.scalar.activation(f_part[h][:], bur[h][:], ACT.Identity, scale=f_bur[:], bias=f_const[:])
-            nc.scalar.activation(g_part[h][:], bur[h][:], ACT.Identity, scale=g_bur[:], bias=g_const[:])
-
-        def make_f(h):
-            nc.vector.scalar_tensor_tensor(f[h][:], skat[h][:], f_skat[:], f_part[h][:], ALU.mult, ALU.add)
-            nc.scalar.activation(gap[h][:], f[h][:], ACT.Abs)
-
-        def make_g(h):
-            nc.vector.scalar_tensor_tensor(g[h][:], skat[h][:], g_skat[:], g_part[h][:], ALU.mult, ALU.add)
-
-        def make_hi(h):
-            nc.vector.scalar_tensor_tensor(hi[h][:], gap[h][:], 0.5, g[h][:], ALU.mult, ALU.add)
-            nc.scalar.activation(hi_abs[h][:], hi[h][:], ACT.Abs)
-            nc.scalar.activation(e_near[h][:], hi_abs[h][:], ACT.Exp, scale=-1.0)
-
-        def make_low(h):
-            nc.vector.scalar_tensor_tensor(low_arg[h][:], hi[h][:], 0.0, gap[h][:], ALU.min, ALU.subtract)
-            nc.scalar.activation(e_low[h][:], low_arg[h][:], ACT.Exp)
-
-        pair_lo(0)
-        pair_hi(0)
-        make_bur(0)
-        pair_lo(1)
-        make_skat(0)
-        make_bur(1)
-        pair_hi(1)
-        make_f(0)
-        make_skat(1)
-        make_g(0)
-        make_f(1)
-        make_hi(0)
-        make_g(1)
-        make_low(0)
-        make_hi(1)
-        make_low(1)
+        lo_pair = before_last
+        for h in halves:
+            add(lo_pair[h], square[0][h][:], square[1][h][:])
+        hi_pair = step("hi_pair", lambda o, h: add(o, square[2][h][:], square[3][h][:]))
+        bur_all = sb("bur", [P, V])
+        for cols in (slice(0, H + 16), slice(H + 16, V)):
+            nc.scalar.activation(bur_all[:, cols], total_all[:, cols], ACT.Square)
+        bur = [bur_all[:, h * H : (h + 1) * H] for h in halves]
+        skat = step("skat", lambda o, h: add(o, lo_pair[h], hi_pair[h][:]))
+        f_part = step("f_part", lambda o, h: nc.scalar.activation(o, bur[h], ACT.Identity, scale=f_bur[:], bias=f_const[:]))
+        g_part = step("g_part", lambda o, h: nc.scalar.activation(o, bur[h], ACT.Identity, scale=g_bur[:], bias=g_const[:]))
+        f = step("f", lambda o, h: fused(o, skat[h][:], f_skat[:], f_part[h][:], ALU.mult, ALU.add))
+        g = step("g", lambda o, h: fused(o, skat[h][:], g_skat[:], g_part[h][:], ALU.mult, ALU.add))
+        gap = step("gap", lambda o, h: nc.scalar.activation(o, f[h][:], ACT.Abs))
+        hi = step("hi", lambda o, h: fused(o, gap[h][:], 0.5, g[h][:], ALU.mult, ALU.add))
+        low_arg = step("low_arg", lambda o, h: fused(o, hi[h][:], 0.0, gap[h][:], ALU.min, ALU.subtract))
+        hi_abs = step("hi_abs", lambda o, h: nc.scalar.activation(o, hi[h][:], ACT.Abs))
+        e_near = step("e_near", lambda o, h: nc.scalar.activation(o, hi_abs[h][:], ACT.Exp, scale=-1.0))
+        e_low = step("e_low", lambda o, h: nc.scalar.activation(o, low_arg[h][:], ACT.Exp))
 
         blocks = range(H // P)
-        rest = []
+        rest = bank("rest", 0, [P, HALVES, H // P, G])
         for h in halves:
-            acc = bank("rest%d" % h, h, [P, H // P, G])
+            acc = rest[:, h]
             for b in blocks:
                 cols = slice(b * P, (b + 1) * P)
                 nc.tensor.matmul(acc[:, b, :], e_near[h][:, cols], ident[:], start=True, stop=False, is_transpose=True)
                 nc.tensor.matmul(acc[:, b, :], e_low[h][:, cols], ident[:], start=False, stop=True, is_transpose=True)
-            rest.append(acc)
 
-        both, z1, top = wide("both"), wide("z1"), wide("top")
+        both, z1, top = gap, wide("z1"), wide("top")
         for h in halves:
-            nc.vector.tensor_tensor(both[h][:], skat[h][:], bur[h][:], ALU.add)
+            nc.vector.tensor_tensor(both[h][:], skat[h][:], bur[h], ALU.add)
         for h in halves:
             nc.vector.tensor_scalar(z1[h][:], both[h][:], z1_factor[:], z1_const[:], ALU.mult, ALU.add)
         top_turned = []
@@ -232,7 +239,7 @@ def tile_picked_yskat_lse_p_kernel(
         out_rows = out.rearrange("(h b p) g -> h p b g", h=HALVES, p=P)
         for h in halves:
             logs = sb("logs%d" % h, [P, H // P, G])
-            nc.scalar.activation(logs[:], rest[h][:], ACT.Ln, bias=1.0)
+            nc.scalar.activation(logs[:], rest[:, h], ACT.Ln, bias=1.0)
             result = sb("result%d" % h, [P, H // P, G])
             nc.vector.tensor_tensor(result[:], top_turned[h][:], logs[:], ALU.add)
             nc.sync.dma_start(out_rows[h], result[:])

@@ -78,12 +78,13 @@ def tile_picked_yskat_lse_p_kernel(
 
         picked_scales = sb("picked_scales", [P, S], U8)
         nc.vector.tensor_copy(picked_scales[:], scale_table[:].indirect(offsets[:]))
+        picked_weights = sb("picked_weights", [P, S])
+        nc.vector.tensor_copy(picked_weights[:], weight_table[:].indirect(offsets[:]))
+
         x_scale = sb("x_scale", [P, S], U8)
         nc.vector.tensor_copy(
             x_scale[:].rearrange("p (d g) -> p d g", d=D), picked_scales[:].rearrange("p (g d) -> p d g", d=D)
         )
-        picked_weights = sb("picked_weights", [P, S])
-        nc.vector.tensor_copy(picked_weights[:], weight_table[:].indirect(offsets[:]))
 
         h_code, h_scale = [], []
 
@@ -113,42 +114,30 @@ def tile_picked_yskat_lse_p_kernel(
         for d in range(D):
             nc.tensor.transpose(turned[:, d, :], picked_weights[:, d:S:D], ident[:])
 
-        i0, i1, i2 = isd
-        recipes = [
-            ("f_skat", 0.0, [(0.9, i0), (-0.1, i2)]),
-            ("f_bur", 0.0, [(0.1, i0), (-0.9, i2)]),
-            ("f_const", 0.0, [(-4.0, i0), (4.0, i2)]),
-            ("g_skat", 0.0, [(0.45, i0), (0.05, i2), (-0.5, i1)]),
-            ("g_bur", 0.0, [(0.05, i0), (0.45, i2), (-0.5, i1)]),
-            ("g_const", 0.0, [(-2.0, i0), (-2.0, i2), (4.0, i1)]),
-            ("z1_factor", 0.0, [(0.5, i1)]),
-            ("z1_const", -math.log(3.0), [(-4.0, i1)]),
-        ]
-        coef = {}
-        for group in (recipes[0:3], recipes[3:6], recipes[6:8]):
-            for n in range(len(group[0][2])):
-                for name, constant, terms in group:
-                    factor, col = terms[n]
-                    nxt = sb("%s_%d" % (name, n), [P, 1])
-                    so_far = constant if n == 0 else coef[name][:]
-                    nc.gpsimd.tensor_scalar(nxt[:], col, factor, so_far, ALU.mult, ALU.add)
-                    coef[name] = nxt
-        f_skat, f_bur, f_const = coef["f_skat"], coef["f_bur"], coef["f_const"]
-        g_skat, g_bur, g_const = coef["g_skat"], coef["g_bur"], coef["g_const"]
-        z1_factor, z1_const = coef["z1_factor"], coef["z1_const"]
-
         x_code = sb("x_code", [P, S], U32)
-        picked_words = sb("picked_words", [P, S], U32)
-        nc.vector.tensor_copy(picked_words[:], word_table[:].indirect(offsets[:]))
-        for pair in range(2):
-            nc.vector.tensor_copy(
-                x_code[:].bitcast(I32).rearrange("p (d g) -> p d g", d=D)[:, 2 * pair : 2 * pair + 2, :],
-                picked_words[:].bitcast(I32).rearrange("p (g d) -> p d g", d=D)[:, 2 * pair : 2 * pair + 2, :],
-            )
+        nc.vector.tensor_copy(x_code[:].rearrange("p (d g) -> p g d", d=D), word_table[:].indirect(offsets[:]))
 
         quantise(1)
-        w = keep.tile([P, D], F32, name="w", tag="h_raw1", align_bytes=64)
-        nc.scalar.copy(w[:], turned[:, :, 0])
+        coef = keep.tile([P, 16], F32, name="coef", tag="h_raw1", align_bytes=64)
+        nc.scalar.copy(coef[:, 0:D], turned[:, :, 0])
+        w = coef[:, 0:D]
+        columns = [coef[:, n : n + 1] for n in range(D, 16)]
+
+        def scaled(factor, col, plus=None):
+            dst = columns.pop()
+            if plus is None:
+                nc.scalar.activation(dst, col, ACT.Copy, scale=factor)
+            else:
+                nc.scalar.activation(dst, col, ACT.Identity, scale=factor, bias=plus)
+            return dst
+
+        i0, i1, i2 = isd
+        minus_half_i1 = scaled(-0.5, i1)
+        f_skat, f_bur = scaled(-0.1, i2), scaled(-0.9, i2)
+        g_skat, g_bur = scaled(0.05, i2, minus_half_i1), scaled(0.45, i2, minus_half_i1)
+        f_skat, f_bur = scaled(0.9, i0, f_skat), scaled(0.1, i0, f_bur)
+        g_skat, g_bur = scaled(0.45, i0, g_skat), scaled(0.05, i0, g_bur)
+        f_const, g_const = scaled(-4.0, f_bur), scaled(-4.0, g_bur)
 
         def wide(name):
             return [sb("%s%d" % (name, h), [P, H]) for h in halves]
@@ -202,11 +191,11 @@ def tile_picked_yskat_lse_p_kernel(
         for cols in (slice(0, H + 16), slice(H + 16, V)):
             nc.scalar.activation(bur_all[:, cols], total_all[:, cols], ACT.Square)
         bur = [bur_all[:, h * H : (h + 1) * H] for h in halves]
-        skat = step("skat", lambda o, h: add(o, lo_pair[h], hi_pair[h][:]))
-        f_part = step("f_part", lambda o, h: nc.scalar.activation(o, bur[h], ACT.Identity, scale=f_bur[:], bias=f_const[:]))
-        g_part = step("g_part", lambda o, h: nc.scalar.activation(o, bur[h], ACT.Identity, scale=g_bur[:], bias=g_const[:]))
-        f = step("f", lambda o, h: fused(o, skat[h][:], f_skat[:], f_part[h][:], ALU.mult, ALU.add))
-        g = step("g", lambda o, h: fused(o, skat[h][:], g_skat[:], g_part[h][:], ALU.mult, ALU.add))
+        skat = step("skat", lambda o, h: fused(o, lo_pair[h], -4.0, hi_pair[h][:], ALU.add, ALU.add))
+        f_part = step("f_part", lambda o, h: nc.scalar.activation(o, bur[h], ACT.Identity, scale=f_bur, bias=f_const))
+        g_part = step("g_part", lambda o, h: nc.scalar.activation(o, bur[h], ACT.Identity, scale=g_bur, bias=g_const))
+        f = step("f", lambda o, h: fused(o, skat[h][:], f_skat, f_part[h][:], ALU.mult, ALU.add))
+        g = step("g", lambda o, h: fused(o, skat[h][:], g_skat, g_part[h][:], ALU.mult, ALU.add))
         gap = step("gap", lambda o, h: nc.scalar.activation(o, f[h][:], ACT.Abs))
         hi = step("hi", lambda o, h: fused(o, gap[h][:], 0.5, g[h][:], ALU.mult, ALU.add))
         low_arg = step("low_arg", lambda o, h: fused(o, hi[h][:], 0.0, gap[h][:], ALU.min, ALU.subtract))
@@ -215,31 +204,33 @@ def tile_picked_yskat_lse_p_kernel(
         e_low = step("e_low", lambda o, h: nc.scalar.activation(o, low_arg[h][:], ACT.Exp))
 
         blocks = range(H // P)
-        rest = bank("rest", 0, [P, HALVES, H // P, G])
+        rest = [bank("rest%d" % b, b, [P, HALVES, G]) for b in blocks]
         for h in halves:
-            acc = rest[:, h]
-            for b in blocks:
-                cols = slice(b * P, (b + 1) * P)
-                nc.tensor.matmul(acc[:, b, :], e_near[h][:, cols], ident[:], start=True, stop=False, is_transpose=True)
-                nc.tensor.matmul(acc[:, b, :], e_low[h][:, cols], ident[:], start=False, stop=True, is_transpose=True)
+            for first, term in ((True, e_near), (False, e_low)):
+                for b in blocks:
+                    nc.tensor.matmul(
+                        rest[b][:, h, :],
+                        term[h][:, b * P : (b + 1) * P],
+                        ident[:],
+                        start=first,
+                        stop=not first,
+                        is_transpose=True,
+                    )
 
-        both, z1, top = gap, wide("z1"), wide("top")
+        both = gap
         for h in halves:
-            nc.vector.tensor_tensor(both[h][:], skat[h][:], bur[h], ALU.add)
+            fused(both[h][:], skat[h][:], -4.0, bur[h], ALU.add, ALU.add)
+        z1 = step("z1", lambda o, h: nc.vector.tensor_scalar(o, both[h][:], i1, 0.5, ALU.mult, ALU.mult))
+        top = step("top", lambda o, h: fused(o, hi[h][:], 0.0, z1[h][:], ALU.max, ALU.add))
+        top_turned = [bank("top_turned%d" % b, 2 + b, [P, HALVES, G]) for b in blocks]
         for h in halves:
-            nc.vector.tensor_scalar(z1[h][:], both[h][:], z1_factor[:], z1_const[:], ALU.mult, ALU.add)
-        top_turned = []
-        for h in halves:
-            nc.vector.scalar_tensor_tensor(top[h][:], hi[h][:], 0.0, z1[h][:], ALU.max, ALU.add)
-            acc = bank("top_turned%d" % h, HALVES + h, [P, H // P, G])
             for b in blocks:
-                nc.tensor.transpose(acc[:, b, :], top[h][:, b * P : (b + 1) * P], ident[:])
-            top_turned.append(acc)
+                nc.tensor.transpose(top_turned[b][:, h, :], top[h][:, b * P : (b + 1) * P], ident[:])
 
-        out_rows = out.rearrange("(h b p) g -> h p b g", h=HALVES, p=P)
-        for h in halves:
-            logs = sb("logs%d" % h, [P, H // P, G])
-            nc.scalar.activation(logs[:], rest[:, h], ACT.Ln, bias=1.0)
-            result = sb("result%d" % h, [P, H // P, G])
-            nc.vector.tensor_tensor(result[:], top_turned[h][:], logs[:], ALU.add)
-            nc.sync.dma_start(out_rows[h], result[:])
+        out_rows = out.rearrange("(h b p) g -> b p h g", h=HALVES, p=P)
+        for b in blocks:
+            logs = sb("logs%d" % b, [P, HALVES, G])
+            nc.scalar.activation(logs[:], rest[b][:], ACT.Ln, bias=1.0)
+            result = sb("result%d" % b, [P, HALVES, G])
+            fused(result[:], top_turned[b][:], -math.log(3.0), logs[:], ALU.add, ALU.add)
+            nc.sync.dma_start(out_rows[b], result[:])

@@ -47,7 +47,7 @@ def tile_picked_yskat_lse_p_kernel(
         nc.sync.dma_start(h_raw0[:], h_rows[:, :, 0:H])
 
         scale_table = sb("scale_table", [P, T], U8)
-        nc.gpsimd.memset(scale_table[:].bitcast(I32), 0)
+        nc.vector.memset(scale_table[:].bitcast(I32), 0)
         for q in range(4):
             nc.sync.dma_start(
                 scale_table[32 * q : 32 * q + 4, :].bitcast(I32), x_scales[0, 4 * q : 4 * q + 4, :].bitcast(I32)
@@ -86,22 +86,21 @@ def tile_picked_yskat_lse_p_kernel(
             x_scale[:].rearrange("p (d g) -> p d g", d=D), picked_scales[:].rearrange("p (g d) -> p d g", d=D)
         )
 
-        h_code, h_scale = [], []
+        h_code = [sb("h_code%d" % h, [P, H], U32) for h in halves]
+        h_scale = [sb("h_scale%d" % h, [P, H], U8) for h in halves]
+        grouped = [sb("h_grouped%d" % h, [P, H, PACK], BF16) for h in halves]
 
-        def quantise(h):
-            grouped = sb("h_grouped%d" % h, [P, H, PACK], BF16)
+        def quantise(h, cols):
             nc.scalar.activation(
-                grouped[:].rearrange("p (c i) j -> p c j i", i=4),
-                h_raw[h][:].rearrange("p j (c i) -> p c j i", i=4),
+                grouped[h][:, cols, :].rearrange("p (c i) j -> p c j i", i=4),
+                h_raw[h][:, :, cols].rearrange("p j (c i) -> p c j i", i=4),
                 ACT.Copy,
             )
-            code = sb("h_code%d" % h, [P, H], U32)
-            scale = sb("h_scale%d" % h, [P, H], U8)
-            nc.vector.quantize_mx(code[:].bitcast(FP8X4), scale[:], grouped[:].rearrange("p c j -> p (c j)"))
-            h_code.append(code)
-            h_scale.append(scale)
+            nc.vector.quantize_mx(
+                h_code[h][:, cols].bitcast(FP8X4), h_scale[h][:, cols], grouped[h][:, cols, :].rearrange("p c j -> p (c j)")
+            )
 
-        quantise(0)
+        quantise(0, slice(0, H))
 
         isd_all = keep.tile([P, 3, 8], F32, name="isd_all", tag="h_raw0", align_bytes=64)
         isd = []
@@ -117,7 +116,8 @@ def tile_picked_yskat_lse_p_kernel(
         x_code = sb("x_code", [P, S], U32)
         nc.vector.tensor_copy(x_code[:].rearrange("p (d g) -> p g d", d=D), word_table[:].indirect(offsets[:]))
 
-        quantise(1)
+        quantise(1, slice(0, H // 2))
+        quantise(1, slice(H // 2, H))
         coef = keep.tile([P, 16], F32, name="coef", tag="h_raw1", align_bytes=64)
         nc.scalar.copy(coef[:, 0:D], turned[:, :, 0])
         w = coef[:, 0:D]
@@ -227,10 +227,11 @@ def tile_picked_yskat_lse_p_kernel(
             for b in blocks:
                 nc.tensor.transpose(top_turned[b][:, h, :], top[h][:, b * P : (b + 1) * P], ident[:])
 
-        out_rows = out.rearrange("(h b p) g -> b p h g", h=HALVES, p=P)
+        out_rows = out.rearrange("(h b p) g -> b h p g", h=HALVES, p=P)
         for b in blocks:
-            logs = sb("logs%d" % b, [P, HALVES, G])
-            nc.scalar.activation(logs[:], rest[b][:], ACT.Ln, bias=1.0)
-            result = sb("result%d" % b, [P, HALVES, G])
-            fused(result[:], top_turned[b][:], -math.log(3.0), logs[:], ALU.add, ALU.add)
-            nc.sync.dma_start(out_rows[b], result[:])
+            for h in halves:
+                logs = sb("logs%d%d" % (b, h), [P, G])
+                nc.scalar.activation(logs[:], rest[b][:, h, :], ACT.Ln, bias=1.0)
+                result = sb("result%d%d" % (b, h), [P, G])
+                fused(result[:], top_turned[b][:, h, :], -math.log(3.0), logs[:], ALU.add, ALU.add)
+                nc.sync.dma_start(out_rows[b, h], result[:])

import math
from contextlib import ExitStack

import concourse.mybir as mybir

K, T, S, V, D, G = 512, 2048, 512, 512, 4, 128
P = 128
PACK = 4
HALVES = 2
H = V // HALVES

FLOPS = 2 * K * V * S
BYTES = K * T + 16 * T + 4 * K * V + 4 * T + 3 * 4 * G + 2 * P * (S // 16) + 4 * V * G

F32 = mybir.dt.float32
BF16 = mybir.dt.bfloat16
I32 = mybir.dt.int32
U32 = mybir.dt.uint32
U16 = mybir.dt.uint16
U8 = mybir.dt.uint8
FP8X4 = mybir.dt.float8_e4m3fn_x4
ALU = mybir.AluOpType
ACT = mybir.ActivationFunctionType


def tile_picked_yskat_lse_p_kernel(
    tc, x_words, x_scales, hT, wgt, isd0, isd1, isd2, offs, out
):
    nc = tc.nc
    with ExitStack() as ctx:
        keep = ctx.enter_context(tc.tile_pool(name="keep", bufs=1))
        psum = ctx.enter_context(tc.psum_pool(name="psum", bufs=1))

        def sb(name, shape, dtype=F32):
            return keep.tile(shape, dtype, name=name, align_bytes=64)

        def bank(name, number, shape):
            return psum.tile(shape, F32, name=name, tag="bank%d" % number)

        halves = range(HALVES)

        offsets = keep.tile([P, S // 16], U16, name="offsets")
        nc.sync.dma_start(offsets[:], offs)

        h_rows = hT.rearrange("(p j) t -> p j t", j=PACK)
        h_raw0 = keep.tile([P, PACK, H], F32, name="h_raw0", tag="h_raw0", align_bytes=64)
        nc.sync.dma_start(h_raw0[:], h_rows[:, :, 0:H])

        scale_table = sb("scale_table", [P, T], U8)
        nc.vector.memset(scale_table[:].bitcast(I32), 0)
        for q in range(4):
            nc.sync.dma_start(
                scale_table[32 * q : 32 * q + 4, :].bitcast(I32), x_scales[0, 4 * q : 4 * q + 4, :].bitcast(I32)
            )

        zero = keep.tile([P, 1], F32, name="zero", tag="word_table", align_bytes=64)
        nc.vector.memset(zero[:], 0.0)
        weight_table = sb("weight_table", [P, T])
        nc.vector.tensor_copy(weight_table[:], zero[:].to_broadcast([P, T]))
        blank = keep.tile([P, P], F32, name="blank", tag="h_raw1", align_bytes=64)
        nc.vector.tensor_copy(blank[:], zero[:].to_broadcast([P, P]))
        ident = sb("ident", [P, P])
        nc.gpsimd.affine_select(
            out=ident[:],
            in_=blank[:],
            compare_op=ALU.not_equal,
            fill=1.0,
            base=0,
            pattern=[[-1, P]],
            channel_multiplier=1,
        )
        nc.sync.dma_start(weight_table[0:1, :], wgt[0:1, :])
        word_table = keep.tile([P, T], U32, name="word_table", tag="word_table", align_bytes=64)
        nc.sync.dma_start(word_table[:].bitcast(I32), x_words[0].rearrange("p n t -> p (n t)").bitcast(I32))
        h_raw1 = keep.tile([P, PACK, H], F32, name="h_raw1", tag="h_raw1", align_bytes=64)
        nc.sync.dma_start(h_raw1[:], h_rows[:, :, H:V])
        h_raw = [h_raw0, h_raw1]

        picked_scales = sb("picked_scales", [P, S], U8)
        nc.vector.tensor_copy(picked_scales[:], scale_table[:].indirect(offsets[:]))
        picked_weights = sb("picked_weights", [P, S])
        nc.vector.tensor_copy(picked_weights[:], weight_table[:].indirect(offsets[:]))

        x_scale = sb("x_scale", [P, S], U8)
        nc.vector.tensor_copy(
            x_scale[:].rearrange("p (d g) -> p d g", d=D), picked_scales[:].rearrange("p (g d) -> p d g", d=D)
        )

        h_code = [sb("h_code%d" % h, [P, H], U32) for h in halves]
        h_scale = [sb("h_scale%d" % h, [P, H], U8) for h in halves]
        grouped = [sb("h_grouped%d" % h, [P, H, PACK], BF16) for h in halves]

        def quantise(h, cols):
            nc.scalar.activation(
                grouped[h][:, cols, :].rearrange("p (c i) j -> p c j i", i=4),
                h_raw[h][:, :, cols].rearrange("p j (c i) -> p c j i", i=4),
                ACT.Copy,
            )
            nc.vector.quantize_mx(
                h_code[h][:, cols].bitcast(FP8X4), h_scale[h][:, cols], grouped[h][:, cols, :].rearrange("p c j -> p (c j)")
            )

        quantise(0, slice(0, H))

        isd_all = keep.tile([P, 3, 8], F32, name="isd_all", tag="h_raw0", align_bytes=64)
        isd = []
        with nc.allow_non_contiguous_dma(reason="one value a partition"):
            for i, src in enumerate((isd0, isd1, isd2)):
                nc.scalar.dma_start(isd_all[:, i, 0:1], src[0:1, :].rearrange("o g -> g o"))
                isd.append(isd_all[:, i, 0:1])

        turned = bank("weights_turned", 7, [P, D, P])
        for d in range(D):
            nc.tensor.transpose(turned[:, d, :], picked_weights[:, d:S:D], ident[:])

        x_code = sb("x_code", [P, S], U32)
        nc.vector.tensor_copy(x_code[:].rearrange("p (d g) -> p g d", d=D), word_table[:].indirect(offsets[:]))

        quantise(1, slice(0, H // 2))
        quantise(1, slice(H // 2, H))
        coef = keep.tile([P, 16], F32, name="coef", tag="h_raw1", align_bytes=64)
        nc.scalar.copy(coef[:, 0:D], turned[:, :, 0])
        w = coef[:, 0:D]
        columns = [coef[:, n : n + 1] for n in range(D, 16)]

        def scaled(factor, col, plus=None):
            dst = columns.pop()
            if plus is None:
                nc.scalar.activation(dst, col, ACT.Copy, scale=factor)
            else:
                nc.scalar.activation(dst, col, ACT.Identity, scale=factor, bias=plus)
            return dst

        i0, i1, i2 = isd
        minus_half_i1 = scaled(-0.5, i1)
        f_skat, f_bur = scaled(-0.1, i2), scaled(-0.9, i2)
        g_skat, g_bur = scaled(0.05, i2, minus_half_i1), scaled(0.45, i2, minus_half_i1)
        f_skat, f_bur = scaled(0.9, i0, f_skat), scaled(0.1, i0, f_bur)
        g_skat, g_bur = scaled(0.45, i0, g_skat), scaled(0.05, i0, g_bur)
        f_const, g_const = scaled(-4.0, f_bur), scaled(-4.0, g_bur)

        def wide(name):
            return [sb("%s%d" % (name, h), [P, H]) for h in halves]

        total = None
        square = []
        for d in range(D):
            total_all = sb("sum%d" % d, [P, V])
            running = [total_all[:, h * H : (h + 1) * H] for h in halves]
            sq = wide("square%d_" % d)
            cols = slice(d * G, (d + 1) * G)
            for h in halves:
                prod = bank("prod%d%d" % (d, h), HALVES * d + h, [P, H])
                nc.tensor.matmul_mx(
                    prod[:],
                    lhsT=x_code[:, cols].bitcast(FP8X4),
                    lhsT_scale=x_scale[:, cols],
                    rhs=h_code[h][:].bitcast(FP8X4),
                    rhs_scale=h_scale[h][:],
                    start=True,
                    stop=True,
                )
                if total is None:
                    nc.vector.tensor_scalar(running[h], prod[:], w[:, d : d + 1], None, ALU.mult)
                else:
                    nc.vector.scalar_tensor_tensor(
                        running[h], prod[:], w[:, d : d + 1], total[h], ALU.mult, ALU.add
                    )
                nc.scalar.activation(sq[h][:], prod[:], ACT.Square, scale=w[:, d : d + 1])
            before_last = total
            total = running
            square.append(sq)

        def step(name, emit):
            tiles = wide(name)
            for h in halves:
                emit(tiles[h][:], h)
            return tiles

        def add(dst, a, b):
            nc.vector.tensor_tensor(dst, a, b, ALU.add)

        def fused(dst, a, scalar, b, op0, op1):
            nc.vector.scalar_tensor_tensor(dst, a, scalar, b, op0, op1)

        lo_pair = before_last
        for h in halves:
            add(lo_pair[h], square[0][h][:], square[1][h][:])
        hi_pair = step("hi_pair", lambda o, h: add(o, square[2][h][:], square[3][h][:]))
        bur_all = sb("bur", [P, V])
        for cols in (slice(0, H + 16), slice(H + 16, V)):
            nc.scalar.activation(bur_all[:, cols], total_all[:, cols], ACT.Square)
        bur = [bur_all[:, h * H : (h + 1) * H] for h in halves]
        skat = step("skat", lambda o, h: fused(o, lo_pair[h], -4.0, hi_pair[h][:], ALU.add, ALU.add))
        f_part = step("f_part", lambda o, h: nc.scalar.activation(o, bur[h], ACT.Identity, scale=f_bur, bias=f_const))
        g_part = step("g_part", lambda o, h: nc.scalar.activation(o, bur[h], ACT.Identity, scale=g_bur, bias=g_const))
        f = step("f", lambda o, h: fused(o, skat[h][:], f_skat, f_part[h][:], ALU.mult, ALU.add))
        g = step("g", lambda o, h: fused(o, skat[h][:], g_skat, g_part[h][:], ALU.mult, ALU.add))
        gap = step("gap", lambda o, h: nc.scalar.activation(o, f[h][:], ACT.Abs))
        hi = step("hi", lambda o, h: fused(o, gap[h][:], 0.5, g[h][:], ALU.mult, ALU.add))
        low_arg = step("low_arg", lambda o, h: fused(o, hi[h][:], 0.0, gap[h][:], ALU.min, ALU.subtract))
        hi_abs = step("hi_abs", lambda o, h: nc.scalar.activation(o, hi[h][:], ACT.Abs))
        e_near = step("e_near", lambda o, h: nc.scalar.activation(o, hi_abs[h][:], ACT.Exp, scale=-1.0))
        e_low = step("e_low", lambda o, h: nc.scalar.activation(o, low_arg[h][:], ACT.Exp))

        blocks = range(H // P)
        rest = [bank("rest%d" % b, b, [P, HALVES, G]) for b in blocks]
        for h in halves:
            for first, term in ((True, e_near), (False, e_low)):
                for b in blocks:
                    nc.tensor.matmul(
                        rest[b][:, h, :],
                        term[h][:, b * P : (b + 1) * P],
                        ident[:],
                        start=first,
                        stop=not first,
                        is_transpose=True,
                    )

        both = gap
        for h in halves:
            fused(both[h][:], skat[h][:], -4.0, bur[h], ALU.add, ALU.add)
        z1 = step("z1", lambda o, h: nc.vector.tensor_scalar(o, both[h][:], i1, 0.5, ALU.mult, ALU.mult))
        top = step("top", lambda o, h: fused(o, hi[h][:], 0.0, z1[h][:], ALU.max, ALU.add))
        top_turned = [bank("top_turned%d" % b, 2 + b, [P, HALVES, G]) for b in blocks]
        for h in halves:
            for b in blocks:
                nc.tensor.transpose(top_turned[b][:, h, :], top[h][:, b * P : (b + 1) * P], ident[:])

        out_rows = out.rearrange("(h b p) g -> b h p g", h=HALVES, p=P)
        for b in blocks:
            for h in halves:
                logs = sb("logs%d%d" % (b, h), [P, G])
                nc.scalar.activation(logs[:], rest[b][:, h, :], ACT.Ln, bias=1.0)
                result = sb("result%d%d" % (b, h), [P, G])
                fused(result[:], top_turned[b][:, h, :], -math.log(3.0), logs[:], ALU.add, ALU.add)
                nc.sync.dma_start(out_rows[b, h], result[:])
